import numpy as np
import ml_dtypes


def mxq(x, axis, fmt="e4m3"):
    dtype, down = {"e4m3": (ml_dtypes.float8_e4m3fn, 7), "e5m2": (ml_dtypes.float8_e5m2, 14)}[fmt]
    v = np.moveaxis(np.asarray(x, np.float32).astype(ml_dtypes.bfloat16).astype(np.float64), axis, -1)
    blocks = v.reshape(v.shape[:-1] + (-1, 32))
    amax = np.abs(blocks).max(-1, keepdims=True)
    byte = np.maximum(np.where(amax > 0, np.frexp(amax)[1] - 1 + 127, 0) - down, 1)
    scale = np.exp2(byte - 127.0)
    codes = (blocks / scale).astype(np.float32).astype(dtype).astype(np.float64)
    return np.moveaxis((codes * scale).reshape(v.shape), -1, axis)


WIDE = False


def mx_kscale(k):
    if not WIDE:
        return np.ones(k)
    levels = np.array([30, -30])
    if k % 512:
        return np.exp2(np.random.permutation(np.resize(levels, k // 32))).repeat(32)
    a = np.empty((k // 512, 16))
    for p in range(k // 512):
        a[p, :8] = np.random.permutation(np.resize(levels, 8))
        for g in range(8):
            far = levels[np.abs(levels - a[p, g]) >= 10]
            a[p, g + 8] = far[np.random.randint(len(far))]
    return np.exp2(a.ravel()).repeat(32)


def f64(x):
    return np.asarray(x).astype(np.float64)


def striped(idx):
    return np.tile(np.asarray(idx).reshape(-1, 16).T, (8, 1)).astype(np.uint16)


def unstriped(offs):
    return offs[:16].T.reshape(-1).astype(np.int64)


E2M1 = np.array([0.0, 0.5, 1.0, 1.5, 2.0, 3.0, 4.0, 6.0, -0.0, -0.5, -1.0, -1.5, -2.0, -3.0, -4.0, -6.0])


def pack_weight(w, fmt):
    k, n = w.shape
    w = f64(np.asarray(w, np.float32).astype(ml_dtypes.bfloat16)).reshape(k // 32, 32, n)
    amax = np.abs(w).max(1)
    if fmt in ("e4m3", "e5m2"):
        byte = np.frexp(amax)[1] - 1 + 127 - (7 if fmt == "e4m3" else 14)
    else:
        mant, ex = np.frexp(amax / 6.0)
        byte = np.where(mant > 0.5, ex, ex - 1) + 127
    byte = np.clip(np.where(amax > 0, byte, 1), 1, 254)
    scaled = (w * np.exp2(127.0 - byte)[:, None, :]).reshape(k, n).astype(np.float32)
    by_word = np.ascontiguousarray(scaled.reshape(k // 512, 128, 4, n).transpose(0, 1, 3, 2))
    if fmt in ("e4m3", "e5m2"):
        words = by_word.astype(ml_dtypes.float8_e4m3fn if fmt == "e4m3" else ml_dtypes.float8_e5m2).view(np.uint8)
    else:
        c = by_word.astype(ml_dtypes.float4_e2m1fn).view(np.uint8) & 0xF
        words = (c[..., 0::2] | (c[..., 1::2] << 4)).reshape(k // 512, 128, 2 * n)
    return np.ascontiguousarray(words), np.ascontiguousarray(byte.astype(np.uint8).reshape(k // 512, 16, n))


def unpack_weight(words, scales, fmt):
    g, _, n = scales.shape
    words = np.ascontiguousarray(words).reshape(g, 128, n, -1)
    if fmt in ("e4m3", "e5m2"):
        vals = words.view(ml_dtypes.float8_e4m3fn if fmt == "e4m3" else ml_dtypes.float8_e5m2).astype(np.float64)
    else:
        nib = np.empty((g, 128, n, 4), np.uint8)
        nib[..., 0::2] = words & 0xF
        nib[..., 1::2] = words >> 4
        vals = E2M1[nib]
    vals = vals * np.repeat(np.exp2(scales.astype(np.float64) - 127.0), 8, axis=1)[..., None]
    return vals.transpose(0, 1, 3, 2).reshape(g * 512, n)


def sigmoid(v):
    return 1.0 / (1.0 + np.exp(-v))


K, T, J, R, O, N, L, E = 512, 2048, 256, 512, 128, 256, 512, 512


def setup_inputs():
    n = np.random.standard_normal
    idx = np.random.permutation(T)[:J]
    idx2 = np.random.permutation(T)[:J]
    idx3 = np.random.permutation(J)[:O]
    idx4 = np.random.permutation(J)[:O]
    idx5 = np.random.permutation(E)[:O]
    fk = mx_kscale(K)
    fr = mx_kscale(R)
    fl = mx_kscale(L)
    xtp = pack_weight(n((K, T)) / fk[:, None], "e2m1")
    wp = pack_weight(n((K, R)) * 1 / np.sqrt(K) * fk[:, None], "e5m2")
    w2p = pack_weight(n((K, R)) * 1 / np.sqrt(K) * fk[:, None] * fr, "e4m3")
    wbp = pack_weight(n((R, N)) * 1 / np.sqrt(R) / fr[:, None], "e4m3")
    sxp = pack_weight(n((L, O)) / fl[:, None], "e5m2")
    wsp = pack_weight(n((L, N)) * 1 / np.sqrt(L) * fl[:, None], "e4m3")
    return {
        "xt_words": xtp[0],
        "xt_scales": xtp[1],
        "w_words": wp[0],
        "w_scales": wp[1],
        "w2_words": w2p[0],
        "w2_scales": w2p[1],
        "sg": (np.random.uniform(0.6, 1.6, (R, 1))).astype(np.float32),
        "bg": (np.random.uniform(-1.0, 1.0, (R, 1))).astype(np.float32),
        "wb_words": wbp[0],
        "wb_scales": wbp[1],
        "sx_words": sxp[0],
        "sx_scales": sxp[1],
        "ws_words": wsp[0],
        "ws_scales": wsp[1],
        "tz": (n((N, E))).astype(np.float32),
        "so": (np.random.uniform(0.6, 1.6, (N, 1))).astype(np.float32),
        "bo": (np.random.uniform(-1.0, 1.0, (N, 1))).astype(np.float32),
        "offs": striped(idx),
        "offs2": striped(idx2),
        "offs3": striped(idx3),
        "offs4": striped(idx4),
        "offs5": striped(idx5),
    }


def reference(xt_words, xt_scales, w_words, w_scales, w2_words, w2_scales, sg, bg, wb_words, wb_scales, sx_words, sx_scales, ws_words, ws_scales, tz, so, bo, offs, offs2, offs3, offs4, offs5):
    idx = unstriped(offs)
    idx2 = unstriped(offs2)
    idx3 = unstriped(offs3)
    idx4 = unstriped(offs4)
    idx5 = unstriped(offs5)
    xtu = unpack_weight(xt_words, xt_scales, "e2m1")
    wu = unpack_weight(w_words, w_scales, "e5m2")
    w2u = unpack_weight(w2_words, w2_scales, "e4m3")
    wbu = unpack_weight(wb_words, wb_scales, "e4m3")
    sxu = unpack_weight(sx_words, sx_scales, "e5m2")
    wsu = unpack_weight(ws_words, ws_scales, "e4m3")
    xtidxg = xtu[:, idx]
    a = wu.T @ xtidxg
    xtidx2g = xtu[:, idx2]
    b = w2u.T @ xtidx2g
    hid = b[:, idx4] * sigmoid(a[:, idx3] * f64(sg) + f64(bg))
    hidq = mxq(hid, 0, "e5m2")
    p = wbu.T @ hidq + wsu.T @ sxu
    y = p * sigmoid(f64(tz)[:, idx5] * f64(so) + f64(bo))
    return y

@@ -1,0 +1,217 @@
+from contextlib import ExitStack
+
+import concourse.mybir as mybir
+
+K, T, J, R, O, N, L, E = 512, 2048, 256, 512, 128, 256, 512, 512
+FLOPS = 2 * (2 * K * R * J + R * N * O + L * N * O)
+
+F32 = mybir.dt.float32
+BF16 = mybir.dt.bfloat16
+I32 = mybir.dt.int32
+U32 = mybir.dt.uint32
+U16 = mybir.dt.uint16
+U8 = mybir.dt.uint8
+E4M3 = mybir.dt.float8_e4m3fn_x4
+E5M2 = mybir.dt.float8_e5m2_x4
+E2M1 = mybir.dt.float4_e2m1fn_x4
+SIGMOID = mybir.ActivationFunctionType.Sigmoid
+MULT = mybir.AluOpType.mult
+
+P = 128
+PACK = 4
+QUADS = 4
+QUAD = 32
+ROWS = 4
+HALVES = N // P
+
+
+def tile_list_ahead_gatefetch_skip_finalgate_kernel(
+    tc, xt_words, xt_scales, w_words, w_scales, w2_words, w2_scales, sg, bg, wb_words, wb_scales,
+    sx_words, sx_scales, ws_words, ws_scales, tz, so, bo, offs, offs2, offs3, offs4, offs5, out,
+):
+    nc = tc.nc
+
+    with ExitStack() as ctx:
+        sb = ctx.enter_context(tc.tile_pool(name="sb", bufs=1))
+        ps = ctx.enter_context(tc.psum_pool(name="ps", bufs=1))
+
+        def tile(name, cols, dtype):
+            return sb.tile([P, cols], dtype, name=name, align_bytes=64)
+
+        def load_list(name, src):
+            lst = sb.tile([P, src.shape[1]], U16, name=name)
+            nc.sync.dma_start(lst[:], src)
+            return lst
+
+        def load_words(name, src):
+            words = tile(name, src.shape[2], U32)
+            nc.sync.dma_start(words[:].bitcast(I32), src[0].rearrange("p c t -> p (c t)").bitcast(I32))
+            return words
+
+        def load_scale_rows(plane, col0, src):
+            cols = src.shape[2]
+            nc.sync.dma_start(plane[0 : QUADS * ROWS, col0 : col0 + cols].bitcast(I32), src[0].bitcast(I32))
+
+        def spread_scale_rows(plane):
+            for q in range(1, QUADS):
+                nc.sync.dma_start(
+                    plane[QUAD * q : QUAD * q + ROWS, :].bitcast(I32),
+                    plane[ROWS * q : ROWS * (q + 1), :].bitcast(I32),
+                )
+
+        xt_plane = tile("xt_plane", T, U8)
+        first_rows = tile("first_rows", 2 * R, U8)
+        second_plane = tile("second_plane", 2 * N + O, U8)
+        for plane in (first_rows, xt_plane, second_plane):
+            nc.vector.memset(plane[:].bitcast(I32), 0)
+
+        list1 = load_list("list1", offs)
+        load_scale_rows(first_rows, 0, w_scales)
+        load_scale_rows(first_rows, R, w2_scales)
+        xt_table = tile("xt_table", T, U16)
+        nc.sync.dma_start(xt_table[:].bitcast(I32), xt_words[0].bitcast(I32))
+        for r in range(ROWS):
+            nc.scalar.dma_start(
+                xt_plane[r:P:QUAD, :].bitcast(I32), xt_scales[0, r : QUADS * ROWS : ROWS, :].bitcast(I32)
+            )
+        sg_cols = tile("sg_cols", PACK, F32)
+        bg_cols = tile("bg_cols", PACK, F32)
+        so_cols = tile("so_cols", HALVES, F32)
+        bo_cols = tile("bo_cols", HALVES, F32)
+        nc.gpsimd.dma_start(sg_cols[:], sg.rearrange("(p t) one -> p (t one)", t=PACK))
+        nc.gpsimd.dma_start(bg_cols[:], bg.rearrange("(p t) one -> p (t one)", t=PACK))
+        with nc.allow_non_contiguous_dma(reason="one value for each partition and half"):
+            nc.gpsimd.dma_start(so_cols[:], so.rearrange("(h p) one -> p (h one)", p=P))
+            nc.gpsimd.dma_start(bo_cols[:], bo.rearrange("(h p) one -> p (h one)", p=P))
+        w_raw = load_words("w_raw", w_words)
+        w2_raw = load_words("w2_raw", w2_words)
+        list2 = load_list("list2", offs2)
+
+        first_plane = tile("first_plane", 2 * R, U8)
+        nc.vector.tensor_copy(
+            first_plane[:].rearrange("p (w t m) -> p w t m", w=2, t=PACK),
+            first_rows[:].rearrange("p (w m t) -> p w t m", w=2, t=PACK),
+        )
+        spread_scale_rows(first_plane)
+
+        list3 = load_list("list3", offs3)
+        list4 = load_list("list4", offs4)
+        load_scale_rows(second_plane, 0, wb_scales)
+        load_scale_rows(second_plane, N, ws_scales)
+        load_scale_rows(second_plane, 2 * N, sx_scales)
+        tz_rows = []
+        for h in range(HALVES):
+            tz_rows.append(tile("tz_rows%d" % h, E, F32))
+            nc.sync.dma_start(tz_rows[h][:], tz[P * h : P * (h + 1), :])
+        list5 = load_list("list5", offs5)
+        wb_codes = load_words("wb_codes", wb_words)
+        ws_codes = load_words("ws_codes", ws_words)
+        sx_codes = load_words("sx_codes", sx_words)
+        spread_scale_rows(second_plane)
+
+        def pick_tokens(name, lst):
+            scales = tile(name + "_scales", J, U8)
+            words = tile(name + "_words", J, U16)
+            nc.vector.tensor_copy(scales[:], xt_plane[:].indirect(lst[:]))
+            nc.vector.tensor_copy(words[:], xt_table[:].indirect(lst[:]))
+            return words, scales
+
+        def deal_columns(name, raw):
+            dealt = tile(name, R, U32)
+            nc.scalar.copy(
+                dealt[:].rearrange("p (t m) -> p t m", t=PACK), raw[:].rearrange("p (m t) -> p t m", t=PACK)
+            )
+            return dealt
+
+        x1_words, x1_scales = pick_tokens("x1", list1)
+        w_codes = deal_columns("w_codes", w_raw)
+        x2_words, x2_scales = pick_tokens("x2", list2)
+        w2_codes = deal_columns("w2_codes", w2_raw)
+
+        a_banks = [ps.tile([P, J], F32, name="a_bank%d" % t) for t in range(PACK)]
+        b_banks = [ps.tile([P, 2 * J], F32, name="b_bank%d" % u) for u in range(PACK // 2)]
+        for t in range(PACK):
+            nc.tensor.matmul_mx(
+                out=a_banks[t][:],
+                lhsT=w_codes[:, P * t : P * (t + 1)].bitcast(E5M2),
+                lhsT_scale=first_plane[:, P * t : P * (t + 1)],
+                rhs=x1_words[:].bitcast(E2M1),
+                rhs_scale=x1_scales[:],
+                start=True,
+                stop=True,
+            )
+        for t in range(PACK):
+            nc.tensor.matmul_mx(
+                out=b_banks[t // 2][:, J * (t % 2) : J * (t % 2 + 1)],
+                lhsT=w2_codes[:, P * t : P * (t + 1)].bitcast(E4M3),
+                lhsT_scale=first_plane[:, R + P * t : R + P * (t + 1)],
+                rhs=x2_words[:].bitcast(E2M1),
+                rhs_scale=x2_scales[:],
+                start=True,
+                stop=True,
+            )
+
+        gates = tile("gates", PACK * O, F32)
+        picked = tile("picked", PACK * O, F32)
+        a_rows = [tile("a_rows%d" % t, J, F32) for t in range(PACK)]
+        b_rows = [tile("b_rows%d" % u, 2 * J, F32) for u in range(PACK // 2)]
+        for t in range(PACK):
+            nc.scalar.copy(a_rows[t][:], a_banks[t][:])
+            nc.scalar.activation(
+                out=gates[:, O * t : O * (t + 1)],
+                in_=a_rows[t][:].indirect(list3[:]),
+                func=SIGMOID,
+                bias=bg_cols[:, t : t + 1],
+                scale=sg_cols[:, t : t + 1],
+            )
+        for u in range(PACK // 2):
+            nc.vector.tensor_copy(b_rows[u][:], b_banks[u][:])
+        for t in range(PACK):
+            nc.vector.tensor_copy(
+                picked[:, O * t : O * (t + 1)],
+                b_rows[t // 2][:, J * (t % 2) : J * (t % 2 + 1)].indirect(list4[:]),
+            )
+
+        hid = tile("hid", O * PACK, BF16)
+        nc.vector.tensor_tensor(
+            hid[:].rearrange("p (o t) -> p o t", t=PACK),
+            picked[:].rearrange("p (t o) -> p o t", t=PACK),
+            gates[:].rearrange("p (t o) -> p o t", t=PACK),
+            MULT,
+        )
+        hid_codes = tile("hid_codes", O, U32)
+        hid_scales = tile("hid_scales", O, U8)
+        nc.vector.quantize_mx(out=hid_codes[:].bitcast(E5M2), scales=hid_scales[:], in_=hid[:])
+
+        for h in range(HALVES):
+            last_gate = tile("last_gate%d" % h, O, F32)
+            nc.scalar.activation(
+                out=last_gate[:],
+                in_=tz_rows[h][:].indirect(list5[:]),
+                func=SIGMOID,
+                bias=bo_cols[:, h : h + 1],
+                scale=so_cols[:, h : h + 1],
+            )
+            p_bank = ps.tile([P, O], F32, name="p_bank%d" % h)
+            nc.tensor.matmul_mx(
+                out=p_bank[:],
+                lhsT=ws_codes[:, P * h : P * (h + 1)].bitcast(E4M3),
+                lhsT_scale=second_plane[:, N + P * h : N + P * (h + 1)],
+                rhs=sx_codes[:].bitcast(E5M2),
+                rhs_scale=second_plane[:, 2 * N : 2 * N + O],
+                start=True,
+                stop=False,
+            )
+            nc.tensor.matmul_mx(
+                out=p_bank[:],
+                lhsT=wb_codes[:, P * h : P * (h + 1)].bitcast(E4M3),
+                lhsT_scale=second_plane[:, P * h : P * (h + 1)],
+                rhs=hid_codes[:].bitcast(E5M2),
+                rhs_scale=hid_scales[:],
+                start=False,
+                stop=True,
+            )
+            result = tile("result%d" % h, O, F32)
+            nc.vector.tensor_tensor(result[:], p_bank[:], last_gate[:], MULT)
+            queue = nc.sync if h == 0 else nc.scalar
+            queue.dma_start(out[P * h : P * (h + 1), :], result[:])

@@ -23,6 +23,7 @@ QUADS = 4
 QUAD = 32
 ROWS = 4
 HALVES = N // P
+BLOCKS = QUADS * ROWS
 
 
 def tile_list_ahead_gatefetch_skip_finalgate_kernel(
@@ -35,79 +36,84 @@ def tile_list_ahead_gatefetch_skip_finalgate_kernel(
         sb = ctx.enter_context(tc.tile_pool(name="sb", bufs=1))
         ps = ctx.enter_context(tc.psum_pool(name="ps", bufs=1))
 
-        def tile(name, cols, dtype):
-            return sb.tile([P, cols], dtype, name=name, align_bytes=64)
+        def tile(name, cols, dtype, tag=None):
+            return sb.tile([P, cols], dtype, name=name, tag=tag or name, align_bytes=64)
 
         def load_list(name, src):
             lst = sb.tile([P, src.shape[1]], U16, name=name)
             nc.sync.dma_start(lst[:], src)
             return lst
 
-        def load_words(name, src):
+        def load_words(queue, name, src):
             words = tile(name, src.shape[2], U32)
-            nc.sync.dma_start(words[:].bitcast(I32), src[0].rearrange("p c t -> p (c t)").bitcast(I32))
+            queue.dma_start(words[:].bitcast(I32), src[0].rearrange("p c t -> p (c t)").bitcast(I32))
             return words
 
-        def load_scale_rows(plane, col0, src):
-            cols = src.shape[2]
-            nc.sync.dma_start(plane[0 : QUADS * ROWS, col0 : col0 + cols].bitcast(I32), src[0].bitcast(I32))
-
-        def spread_scale_rows(plane):
-            for q in range(1, QUADS):
-                nc.sync.dma_start(
-                    plane[QUAD * q : QUAD * q + ROWS, :].bitcast(I32),
-                    plane[ROWS * q : ROWS * (q + 1), :].bitcast(I32),
-                )
+        def load_scale_rows(queue, rows, src):
+            queue.dma_start(rows.bitcast(I32), src[0].bitcast(I32))
 
         xt_plane = tile("xt_plane", T, U8)
-        first_rows = tile("first_rows", 2 * R, U8)
+        first_rows = tile("first_rows", R, U8)
+        first_plane = tile("first_plane", 2 * R, U8)
         second_plane = tile("second_plane", 2 * N + O, U8)
-        for plane in (first_rows, xt_plane, second_plane):
-            nc.vector.memset(plane[:].bitcast(I32), 0)
+        for plane in (xt_plane[:], first_rows[QUAD : 2 * QUAD, :], first_rows[2 * QUAD : P, :], first_plane[:], second_plane[:]):
+            nc.vector.memset(plane.bitcast(I32), 0)
 
-        list1 = load_list("list1", offs)
-        load_scale_rows(first_rows, 0, w_scales)
-        load_scale_rows(first_rows, R, w2_scales)
+        load_scale_rows(nc.sync, first_rows[0 : 2 * BLOCKS : 2, :], w_scales)
+        load_scale_rows(nc.sync, first_rows[1 : 2 * BLOCKS : 2, :], w2_scales)
         xt_table = tile("xt_table", T, U16)
         nc.sync.dma_start(xt_table[:].bitcast(I32), xt_words[0].bitcast(I32))
+        list1 = load_list("list1", offs)
         for r in range(ROWS):
-            nc.scalar.dma_start(
-                xt_plane[r:P:QUAD, :].bitcast(I32), xt_scales[0, r : QUADS * ROWS : ROWS, :].bitcast(I32)
-            )
-        sg_cols = tile("sg_cols", PACK, F32)
-        bg_cols = tile("bg_cols", PACK, F32)
-        so_cols = tile("so_cols", HALVES, F32)
-        bo_cols = tile("bo_cols", HALVES, F32)
-        nc.gpsimd.dma_start(sg_cols[:], sg.rearrange("(p t) one -> p (t one)", t=PACK))
-        nc.gpsimd.dma_start(bg_cols[:], bg.rearrange("(p t) one -> p (t one)", t=PACK))
-        with nc.allow_non_contiguous_dma(reason="one value for each partition and half"):
-            nc.gpsimd.dma_start(so_cols[:], so.rearrange("(h p) one -> p (h one)", p=P))
-            nc.gpsimd.dma_start(bo_cols[:], bo.rearrange("(h p) one -> p (h one)", p=P))
-        w_raw = load_words("w_raw", w_words)
-        w2_raw = load_words("w2_raw", w2_words)
+            nc.scalar.dma_start(xt_plane[r:P:QUAD, :].bitcast(I32), xt_scales[0, r:BLOCKS:ROWS, :].bitcast(I32))
         list2 = load_list("list2", offs2)
-
-        first_plane = tile("first_plane", 2 * R, U8)
-        nc.vector.tensor_copy(
-            first_plane[:].rearrange("p (w t m) -> p w t m", w=2, t=PACK),
-            first_rows[:].rearrange("p (w m t) -> p w t m", w=2, t=PACK),
-        )
-        spread_scale_rows(first_plane)
-
+        w2_raw = load_words(nc.sync, "w2_raw", w2_words)
         list3 = load_list("list3", offs3)
         list4 = load_list("list4", offs4)
-        load_scale_rows(second_plane, 0, wb_scales)
-        load_scale_rows(second_plane, N, ws_scales)
-        load_scale_rows(second_plane, 2 * N, sx_scales)
+        warm = tile("warm", 1, F32)
+        warm_out = tile("warm_out", 1, F32)
+        nc.vector.memset(warm[:], 0.0)
+        nc.scalar.activation(out=warm_out[:], in_=warm[:], func=SIGMOID)
+
+        sg_cols = tile("sg_cols", PACK, F32)
+        bg_cols = tile("bg_cols", PACK, F32)
+        w_raw = load_words(nc.gpsimd, "w_raw", w_words)
+        nc.gpsimd.dma_start(sg_cols[:], sg.rearrange("(p t) one -> p (t one)", t=PACK))
+        nc.gpsimd.dma_start(bg_cols[:], bg.rearrange("(p t) one -> p (t one)", t=PACK))
+        sx_codes = load_words(nc.gpsimd, "sx_codes", sx_words)
+
+        dealt_rows = tile("dealt_rows", R, U8)
+        nc.vector.tensor_copy(
+            dealt_rows[:].rearrange("p (t m) -> p t m", t=PACK),
+            first_rows[:].rearrange("p (m t) -> p t m", t=PACK),
+        )
+        for q in range(QUADS):
+            queue = nc.scalar if q == 0 else nc.sync
+            queue.dma_start(
+                first_plane[QUAD * q : QUAD * q + ROWS, :].bitcast(I32).rearrange("r (w c) -> r w c", w=2),
+                dealt_rows[2 * ROWS * q : 2 * ROWS * (q + 1), :].bitcast(I32),
+            )
+
+        load_scale_rows(nc.sync, second_plane[0:BLOCKS, 0:N], wb_scales)
+        load_scale_rows(nc.sync, second_plane[0:BLOCKS, 2 * N : 2 * N + O], sx_scales)
+        load_scale_rows(nc.sync, second_plane[0:BLOCKS, N : 2 * N], ws_scales)
+        so_cols = tile("so_cols", HALVES, F32)
+        bo_cols = tile("bo_cols", HALVES, F32)
+        with nc.allow_non_contiguous_dma(reason="one value for each partition and half"):
+            nc.sync.dma_start(so_cols[:], so.rearrange("(h p) one -> p (h one)", p=P))
+            nc.sync.dma_start(bo_cols[:], bo.rearrange("(h p) one -> p (h one)", p=P))
         tz_rows = []
         for h in range(HALVES):
             tz_rows.append(tile("tz_rows%d" % h, E, F32))
             nc.sync.dma_start(tz_rows[h][:], tz[P * h : P * (h + 1), :])
         list5 = load_list("list5", offs5)
-        wb_codes = load_words("wb_codes", wb_words)
-        ws_codes = load_words("ws_codes", ws_words)
-        sx_codes = load_words("sx_codes", sx_words)
-        spread_scale_rows(second_plane)
+        wb_codes = load_words(nc.sync, "wb_codes", wb_words)
+        ws_codes = load_words(nc.sync, "ws_codes", ws_words)
+        for q in range(1, QUADS):
+            nc.sync.dma_start(
+                second_plane[QUAD * q : QUAD * q + ROWS, :].bitcast(I32),
+                second_plane[ROWS * q : ROWS * (q + 1), :].bitcast(I32),
+            )
 
         def pick_tokens(name, lst):
             scales = tile(name + "_scales", J, U8)
@@ -116,23 +122,27 @@ def tile_list_ahead_gatefetch_skip_finalgate_kernel(
             nc.vector.tensor_copy(words[:], xt_table[:].indirect(lst[:]))
             return words, scales
 
-        def deal_columns(name, raw):
-            dealt = tile(name, R, U32)
+        def deal_columns(name, raw, tag=None):
+            dealt = tile(name, R, U32, tag)
             nc.scalar.copy(
-                dealt[:].rearrange("p (t m) -> p t m", t=PACK), raw[:].rearrange("p (m t) -> p t m", t=PACK)
+                dealt[:].rearrange("p (t m) -> p m t", t=PACK), raw[:].rearrange("p (m t) -> p m t", t=PACK)
             )
             return dealt
 
         x1_words, x1_scales = pick_tokens("x1", list1)
-        w_codes = deal_columns("w_codes", w_raw)
+        w_codes = deal_columns("w_codes", w_raw, "first_rows")
         x2_words, x2_scales = pick_tokens("x2", list2)
         w2_codes = deal_columns("w2_codes", w2_raw)
 
-        a_banks = [ps.tile([P, J], F32, name="a_bank%d" % t) for t in range(PACK)]
-        b_banks = [ps.tile([P, 2 * J], F32, name="b_bank%d" % u) for u in range(PACK // 2)]
-        for t in range(PACK):
+        gates = tile("gates", PACK * O, F32)
+        picked = tile("picked", PACK * O, F32)
+        a_rows = [tile("a_rows%d" % t, J, F32) for t in range(PACK)]
+        b_rows = [tile("b_rows%d" % t, J, F32) for t in range(PACK)]
+
+        def multiply(t):
+            a_bank = ps.tile([P, J], F32, name="a_bank%d" % t, tag="a_bank%d" % t)
             nc.tensor.matmul_mx(
-                out=a_banks[t][:],
+                out=a_bank[:],
                 lhsT=w_codes[:, P * t : P * (t + 1)].bitcast(E5M2),
                 lhsT_scale=first_plane[:, P * t : P * (t + 1)],
                 rhs=x1_words[:].bitcast(E2M1),
@@ -140,9 +150,9 @@ def tile_list_ahead_gatefetch_skip_finalgate_kernel(
                 start=True,
                 stop=True,
             )
-        for t in range(PACK):
+            b_bank = ps.tile([P, J], F32, name="b_bank%d" % t, tag="b_bank%d" % t)
             nc.tensor.matmul_mx(
-                out=b_banks[t // 2][:, J * (t % 2) : J * (t % 2 + 1)],
+                out=b_bank[:],
                 lhsT=w2_codes[:, P * t : P * (t + 1)].bitcast(E4M3),
                 lhsT_scale=first_plane[:, R + P * t : R + P * (t + 1)],
                 rhs=x2_words[:].bitcast(E2M1),
@@ -150,13 +160,10 @@ def tile_list_ahead_gatefetch_skip_finalgate_kernel(
                 start=True,
                 stop=True,
             )
+            nc.scalar.copy(a_rows[t][:], a_bank[:])
+            nc.vector.tensor_copy(b_rows[t][:], b_bank[:])
 
-        gates = tile("gates", PACK * O, F32)
-        picked = tile("picked", PACK * O, F32)
-        a_rows = [tile("a_rows%d" % t, J, F32) for t in range(PACK)]
-        b_rows = [tile("b_rows%d" % u, 2 * J, F32) for u in range(PACK // 2)]
-        for t in range(PACK):
-            nc.scalar.copy(a_rows[t][:], a_banks[t][:])
+        def look_up(t):
             nc.scalar.activation(
                 out=gates[:, O * t : O * (t + 1)],
                 in_=a_rows[t][:].indirect(list3[:]),
@@ -164,19 +171,19 @@ def tile_list_ahead_gatefetch_skip_finalgate_kernel(
                 bias=bg_cols[:, t : t + 1],
                 scale=sg_cols[:, t : t + 1],
             )
-        for u in range(PACK // 2):
-            nc.vector.tensor_copy(b_rows[u][:], b_banks[u][:])
-        for t in range(PACK):
-            nc.vector.tensor_copy(
-                picked[:, O * t : O * (t + 1)],
-                b_rows[t // 2][:, J * (t % 2) : J * (t % 2 + 1)].indirect(list4[:]),
-            )
+            nc.vector.tensor_copy(picked[:, O * t : O * (t + 1)], b_rows[t][:].indirect(list4[:]))
+
+        multiply(0)
+        for t in range(1, PACK):
+            multiply(t)
+            look_up(t - 1)
+        look_up(PACK - 1)
 
         hid = tile("hid", O * PACK, BF16)
         nc.vector.tensor_tensor(
-            hid[:].rearrange("p (o t) -> p o t", t=PACK),
-            picked[:].rearrange("p (t o) -> p o t", t=PACK),
-            gates[:].rearrange("p (t o) -> p o t", t=PACK),
+            hid[:].rearrange("p (c i t) -> p c t i", i=PACK, t=PACK),
+            picked[:].rearrange("p (t c i) -> p c t i", t=PACK, i=PACK),
+            gates[:].rearrange("p (t c i) -> p c t i", t=PACK, i=PACK),
             MULT,
         )
         hid_codes = tile("hid_codes", O, U32)
@@ -192,7 +199,7 @@ def tile_list_ahead_gatefetch_skip_finalgate_kernel(
                 bias=bo_cols[:, h : h + 1],
                 scale=so_cols[:, h : h + 1],
             )
-            p_bank = ps.tile([P, O], F32, name="p_bank%d" % h)
+            p_bank = ps.tile([P, O], F32, name="p_bank%d" % h, tag="a_bank%d" % h)
             nc.tensor.matmul_mx(
                 out=p_bank[:],
                 lhsT=ws_codes[:, P * h : P * (h + 1)].bitcast(E4M3),

@@ -22,8 +22,9 @@ PACK = 4
 QUADS = 4
 QUAD = 32
 ROWS = 4
-HALVES = N // P
 BLOCKS = QUADS * ROWS
+HALVES = N // P
+LINE = 4
 
 
 def tile_list_ahead_gatefetch_skip_finalgate_kernel(
@@ -56,20 +57,27 @@ def tile_list_ahead_gatefetch_skip_finalgate_kernel(
         first_rows = tile("first_rows", R, U8)
         first_plane = tile("first_plane", 2 * R, U8)
         second_plane = tile("second_plane", 2 * N + O, U8)
-        for plane in (xt_plane[:], first_rows[QUAD : 2 * QUAD, :], first_rows[2 * QUAD : P, :], first_plane[:], second_plane[:]):
-            nc.vector.memset(plane.bitcast(I32), 0)
+        for zeroed in (
+            xt_plane[:],
+            first_rows[QUAD : 2 * QUAD, :],
+            first_rows[2 * QUAD : P, :],
+            first_plane[:],
+            second_plane[:],
+        ):
+            nc.vector.memset(zeroed.bitcast(I32), 0)
 
         load_scale_rows(nc.sync, first_rows[0 : 2 * BLOCKS : 2, :], w_scales)
         load_scale_rows(nc.sync, first_rows[1 : 2 * BLOCKS : 2, :], w2_scales)
-        xt_table = tile("xt_table", T, U16)
-        nc.sync.dma_start(xt_table[:].bitcast(I32), xt_words[0].bitcast(I32))
         list1 = load_list("list1", offs)
         for r in range(ROWS):
-            nc.scalar.dma_start(xt_plane[r:P:QUAD, :].bitcast(I32), xt_scales[0, r:BLOCKS:ROWS, :].bitcast(I32))
+            queue = nc.scalar if r < ROWS // 2 else nc.sync
+            queue.dma_start(xt_plane[r:P:QUAD, :].bitcast(I32), xt_scales[0, r:BLOCKS:ROWS, :].bitcast(I32))
+        xt_table = tile("xt_table", T, U16)
+        nc.sync.dma_start(xt_table[:].bitcast(I32), xt_words[0].bitcast(I32))
         list2 = load_list("list2", offs2)
         w2_raw = load_words(nc.sync, "w2_raw", w2_words)
         list3 = load_list("list3", offs3)
-        list4 = load_list("list4", offs4)
+
         warm = tile("warm", 1, F32)
         warm_out = tile("warm_out", 1, F32)
         nc.vector.memset(warm[:], 0.0)
@@ -93,6 +101,8 @@ def tile_list_ahead_gatefetch_skip_finalgate_kernel(
                 first_plane[QUAD * q : QUAD * q + ROWS, :].bitcast(I32).rearrange("r (w c) -> r w c", w=2),
                 dealt_rows[2 * ROWS * q : 2 * ROWS * (q + 1), :].bitcast(I32),
             )
+
+        list4 = load_list("list4", offs4)
 
         load_scale_rows(nc.sync, second_plane[0:BLOCKS, 0:N], wb_scales)
         load_scale_rows(nc.sync, second_plane[0:BLOCKS, 2 * N : 2 * N + O], sx_scales)
@@ -139,51 +149,53 @@ def tile_list_ahead_gatefetch_skip_finalgate_kernel(
         a_rows = [tile("a_rows%d" % t, J, F32) for t in range(PACK)]
         b_rows = [tile("b_rows%d" % t, J, F32) for t in range(PACK)]
 
-        def multiply(t):
-            a_bank = ps.tile([P, J], F32, name="a_bank%d" % t, tag="a_bank%d" % t)
-            nc.tensor.matmul_mx(
-                out=a_bank[:],
-                lhsT=w_codes[:, P * t : P * (t + 1)].bitcast(E5M2),
-                lhsT_scale=first_plane[:, P * t : P * (t + 1)],
-                rhs=x1_words[:].bitcast(E2M1),
-                rhs_scale=x1_scales[:],
-                start=True,
-                stop=True,
-            )
-            b_bank = ps.tile([P, J], F32, name="b_bank%d" % t, tag="b_bank%d" % t)
-            nc.tensor.matmul_mx(
-                out=b_bank[:],
-                lhsT=w2_codes[:, P * t : P * (t + 1)].bitcast(E4M3),
-                lhsT_scale=first_plane[:, R + P * t : R + P * (t + 1)],
-                rhs=x2_words[:].bitcast(E2M1),
-                rhs_scale=x2_scales[:],
-                start=True,
-                stop=True,
-            )
-            nc.scalar.copy(a_rows[t][:], a_bank[:])
-            nc.vector.tensor_copy(b_rows[t][:], b_bank[:])
+        def gate_rows(row_sets):
+            for t in row_sets:
+                a_bank = ps.tile([P, J], F32, name="a_bank%d" % t, tag="a_bank%d" % t)
+                nc.tensor.matmul_mx(
+                    out=a_bank[:],
+                    lhsT=w_codes[:, P * t : P * (t + 1)].bitcast(E5M2),
+                    lhsT_scale=first_plane[:, P * t : P * (t + 1)],
+                    rhs=x1_words[:].bitcast(E2M1),
+                    rhs_scale=x1_scales[:],
+                    start=True,
+                    stop=True,
+                )
+                nc.scalar.copy(a_rows[t][:], a_bank[:])
+            for t in row_sets:
+                nc.scalar.activation(
+                    out=gates[:, O * t : O * (t + 1)],
+                    in_=a_rows[t][:].indirect(list3[:]),
+                    func=SIGMOID,
+                    bias=bg_cols[:, t : t + 1],
+                    scale=sg_cols[:, t : t + 1],
+                )
 
-        def look_up(t):
-            nc.scalar.activation(
-                out=gates[:, O * t : O * (t + 1)],
-                in_=a_rows[t][:].indirect(list3[:]),
-                func=SIGMOID,
-                bias=bg_cols[:, t : t + 1],
-                scale=sg_cols[:, t : t + 1],
-            )
-            nc.vector.tensor_copy(picked[:, O * t : O * (t + 1)], b_rows[t][:].indirect(list4[:]))
+        def value_rows(row_sets):
+            for t in row_sets:
+                b_bank = ps.tile([P, J], F32, name="b_bank%d" % t, tag="b_bank%d" % t)
+                nc.tensor.matmul_mx(
+                    out=b_bank[:],
+                    lhsT=w2_codes[:, P * t : P * (t + 1)].bitcast(E4M3),
+                    lhsT_scale=first_plane[:, R + P * t : R + P * (t + 1)],
+                    rhs=x2_words[:].bitcast(E2M1),
+                    rhs_scale=x2_scales[:],
+                    start=True,
+                    stop=True,
+                )
+                nc.vector.tensor_copy(b_rows[t][:], b_bank[:])
+            for t in row_sets:
+                nc.vector.tensor_copy(picked[:, O * t : O * (t + 1)], b_rows[t][:].indirect(list4[:]))
 
-        multiply(0)
-        for t in range(1, PACK):
-            multiply(t)
-            look_up(t - 1)
-        look_up(PACK - 1)
+        gate_rows(range(0, PACK // 2))
+        value_rows(range(PACK))
+        gate_rows(range(PACK // 2, PACK))
 
         hid = tile("hid", O * PACK, BF16)
         nc.vector.tensor_tensor(
-            hid[:].rearrange("p (c i t) -> p c t i", i=PACK, t=PACK),
-            picked[:].rearrange("p (t c i) -> p c t i", t=PACK, i=PACK),
-            gates[:].rearrange("p (t c i) -> p c t i", t=PACK, i=PACK),
+            hid[:].rearrange("p (c i t) -> p c t i", i=LINE, t=PACK),
+            picked[:].rearrange("p (t c i) -> p c t i", t=PACK, i=LINE),
+            gates[:].rearrange("p (t c i) -> p c t i", t=PACK, i=LINE),
             MULT,
         )
         hid_codes = tile("hid_codes", O, U32)

from contextlib import ExitStack

import concourse.mybir as mybir

K, T, J, R, O, N, L, E = 512, 2048, 256, 512, 128, 256, 512, 512
FLOPS = 2 * (2 * K * R * J + R * N * O + L * N * O)

F32 = mybir.dt.float32
BF16 = mybir.dt.bfloat16
I32 = mybir.dt.int32
U32 = mybir.dt.uint32
U16 = mybir.dt.uint16
U8 = mybir.dt.uint8
E4M3 = mybir.dt.float8_e4m3fn_x4
E5M2 = mybir.dt.float8_e5m2_x4
E2M1 = mybir.dt.float4_e2m1fn_x4
SIGMOID = mybir.ActivationFunctionType.Sigmoid
MULT = mybir.AluOpType.mult

P = 128
PACK = 4
QUADS = 4
QUAD = 32
ROWS = 4
BLOCKS = QUADS * ROWS
HALVES = N // P
LINE = 4


def tile_list_ahead_gatefetch_skip_finalgate_kernel(
    tc, xt_words, xt_scales, w_words, w_scales, w2_words, w2_scales, sg, bg, wb_words, wb_scales,
    sx_words, sx_scales, ws_words, ws_scales, tz, so, bo, offs, offs2, offs3, offs4, offs5, out,
):
    nc = tc.nc

    with ExitStack() as ctx:
        sb = ctx.enter_context(tc.tile_pool(name="sb", bufs=1))
        ps = ctx.enter_context(tc.psum_pool(name="ps", bufs=1))

        def tile(name, cols, dtype, tag=None):
            return sb.tile([P, cols], dtype, name=name, tag=tag or name, align_bytes=64)

        def load_list(name, src):
            lst = sb.tile([P, src.shape[1]], U16, name=name)
            nc.sync.dma_start(lst[:], src)
            return lst

        def load_words(queue, name, src):
            words = tile(name, src.shape[2], U32)
            queue.dma_start(words[:].bitcast(I32), src[0].rearrange("p c t -> p (c t)").bitcast(I32))
            return words

        def load_scale_rows(queue, rows, src):
            queue.dma_start(rows.bitcast(I32), src[0].bitcast(I32))

        xt_plane = tile("xt_plane", T, U8)
        first_rows = tile("first_rows", R, U8)
        first_plane = tile("first_plane", 2 * R, U8)
        second_plane = tile("second_plane", 2 * N + O, U8)
        for zeroed in (
            xt_plane[:],
            first_rows[QUAD : 2 * QUAD, :],
            first_rows[2 * QUAD : P, :],
            first_plane[:],
            second_plane[:],
        ):
            nc.vector.memset(zeroed.bitcast(I32), 0)

        load_scale_rows(nc.sync, first_rows[0 : 2 * BLOCKS : 2, :], w_scales)
        load_scale_rows(nc.sync, first_rows[1 : 2 * BLOCKS : 2, :], w2_scales)
        list1 = load_list("list1", offs)
        for r in range(ROWS):
            queue = nc.scalar if r < ROWS // 2 else nc.sync
            queue.dma_start(xt_plane[r:P:QUAD, :].bitcast(I32), xt_scales[0, r:BLOCKS:ROWS, :].bitcast(I32))
        xt_table = tile("xt_table", T, U16)
        nc.sync.dma_start(xt_table[:].bitcast(I32), xt_words[0].bitcast(I32))
        list2 = load_list("list2", offs2)
        w2_raw = load_words(nc.sync, "w2_raw", w2_words)
        list3 = load_list("list3", offs3)

        warm = tile("warm", 1, F32)
        warm_out = tile("warm_out", 1, F32)
        nc.vector.memset(warm[:], 0.0)
        nc.scalar.activation(out=warm_out[:], in_=warm[:], func=SIGMOID)

        sg_cols = tile("sg_cols", PACK, F32)
        bg_cols = tile("bg_cols", PACK, F32)
        w_raw = load_words(nc.gpsimd, "w_raw", w_words)
        nc.gpsimd.dma_start(sg_cols[:], sg.rearrange("(p t) one -> p (t one)", t=PACK))
        nc.gpsimd.dma_start(bg_cols[:], bg.rearrange("(p t) one -> p (t one)", t=PACK))
        sx_codes = load_words(nc.gpsimd, "sx_codes", sx_words)

        dealt_rows = tile("dealt_rows", R, U8)
        nc.vector.tensor_copy(
            dealt_rows[:].rearrange("p (t m) -> p t m", t=PACK),
            first_rows[:].rearrange("p (m t) -> p t m", t=PACK),
        )
        for q in range(QUADS):
            queue = nc.scalar if q == 0 else nc.sync
            queue.dma_start(
                first_plane[QUAD * q : QUAD * q + ROWS, :].bitcast(I32).rearrange("r (w c) -> r w c", w=2),
                dealt_rows[2 * ROWS * q : 2 * ROWS * (q + 1), :].bitcast(I32),
            )

        list4 = load_list("list4", offs4)

        load_scale_rows(nc.sync, second_plane[0:BLOCKS, 0:N], wb_scales)
        load_scale_rows(nc.sync, second_plane[0:BLOCKS, 2 * N : 2 * N + O], sx_scales)
        load_scale_rows(nc.sync, second_plane[0:BLOCKS, N : 2 * N], ws_scales)
        so_cols = tile("so_cols", HALVES, F32)
        bo_cols = tile("bo_cols", HALVES, F32)
        with nc.allow_non_contiguous_dma(reason="one value for each partition and half"):
            nc.sync.dma_start(so_cols[:], so.rearrange("(h p) one -> p (h one)", p=P))
            nc.sync.dma_start(bo_cols[:], bo.rearrange("(h p) one -> p (h one)", p=P))
        tz_rows = []
        for h in range(HALVES):
            tz_rows.append(tile("tz_rows%d" % h, E, F32))
            nc.sync.dma_start(tz_rows[h][:], tz[P * h : P * (h + 1), :])
        list5 = load_list("list5", offs5)
        wb_codes = load_words(nc.sync, "wb_codes", wb_words)
        ws_codes = load_words(nc.sync, "ws_codes", ws_words)
        for q in range(1, QUADS):
            nc.sync.dma_start(
                second_plane[QUAD * q : QUAD * q + ROWS, :].bitcast(I32),
                second_plane[ROWS * q : ROWS * (q + 1), :].bitcast(I32),
            )

        def pick_tokens(name, lst):
            scales = tile(name + "_scales", J, U8)
            words = tile(name + "_words", J, U16)
            nc.vector.tensor_copy(scales[:], xt_plane[:].indirect(lst[:]))
            nc.vector.tensor_copy(words[:], xt_table[:].indirect(lst[:]))
            return words, scales

        def deal_columns(name, raw, tag=None):
            dealt = tile(name, R, U32, tag)
            nc.scalar.copy(
                dealt[:].rearrange("p (t m) -> p m t", t=PACK), raw[:].rearrange("p (m t) -> p m t", t=PACK)
            )
            return dealt

        x1_words, x1_scales = pick_tokens("x1", list1)
        w_codes = deal_columns("w_codes", w_raw, "first_rows")
        x2_words, x2_scales = pick_tokens("x2", list2)
        w2_codes = deal_columns("w2_codes", w2_raw)

        gates = tile("gates", PACK * O, F32)
        picked = tile("picked", PACK * O, F32)
        a_rows = [tile("a_rows%d" % t, J, F32) for t in range(PACK)]
        b_rows = [tile("b_rows%d" % t, J, F32) for t in range(PACK)]

        def gate_rows(row_sets):
            for t in row_sets:
                a_bank = ps.tile([P, J], F32, name="a_bank%d" % t, tag="a_bank%d" % t)
                nc.tensor.matmul_mx(
                    out=a_bank[:],
                    lhsT=w_codes[:, P * t : P * (t + 1)].bitcast(E5M2),
                    lhsT_scale=first_plane[:, P * t : P * (t + 1)],
                    rhs=x1_words[:].bitcast(E2M1),
                    rhs_scale=x1_scales[:],
                    start=True,
                    stop=True,
                )
                nc.scalar.copy(a_rows[t][:], a_bank[:])
            for t in row_sets:
                nc.scalar.activation(
                    out=gates[:, O * t : O * (t + 1)],
                    in_=a_rows[t][:].indirect(list3[:]),
                    func=SIGMOID,
                    bias=bg_cols[:, t : t + 1],
                    scale=sg_cols[:, t : t + 1],
                )

        def value_rows(row_sets):
            for t in row_sets:
                b_bank = ps.tile([P, J], F32, name="b_bank%d" % t, tag="b_bank%d" % t)
                nc.tensor.matmul_mx(
                    out=b_bank[:],
                    lhsT=w2_codes[:, P * t : P * (t + 1)].bitcast(E4M3),
                    lhsT_scale=first_plane[:, R + P * t : R + P * (t + 1)],
                    rhs=x2_words[:].bitcast(E2M1),
                    rhs_scale=x2_scales[:],
                    start=True,
                    stop=True,
                )
                nc.vector.tensor_copy(b_rows[t][:], b_bank[:])
            for t in row_sets:
                nc.vector.tensor_copy(picked[:, O * t : O * (t + 1)], b_rows[t][:].indirect(list4[:]))

        gate_rows(range(0, PACK // 2))
        value_rows(range(PACK))
        gate_rows(range(PACK // 2, PACK))

        hid = tile("hid", O * PACK, BF16)
        nc.vector.tensor_tensor(
            hid[:].rearrange("p (c i t) -> p c t i", i=LINE, t=PACK),
            picked[:].rearrange("p (t c i) -> p c t i", t=PACK, i=LINE),
            gates[:].rearrange("p (t c i) -> p c t i", t=PACK, i=LINE),
            MULT,
        )
        hid_codes = tile("hid_codes", O, U32)
        hid_scales = tile("hid_scales", O, U8)
        nc.vector.quantize_mx(out=hid_codes[:].bitcast(E5M2), scales=hid_scales[:], in_=hid[:])

        for h in range(HALVES):
            last_gate = tile("last_gate%d" % h, O, F32)
            nc.scalar.activation(
                out=last_gate[:],
                in_=tz_rows[h][:].indirect(list5[:]),
                func=SIGMOID,
                bias=bo_cols[:, h : h + 1],
                scale=so_cols[:, h : h + 1],
            )
            p_bank = ps.tile([P, O], F32, name="p_bank%d" % h, tag="a_bank%d" % h)
            nc.tensor.matmul_mx(
                out=p_bank[:],
                lhsT=ws_codes[:, P * h : P * (h + 1)].bitcast(E4M3),
                lhsT_scale=second_plane[:, N + P * h : N + P * (h + 1)],
                rhs=sx_codes[:].bitcast(E5M2),
                rhs_scale=second_plane[:, 2 * N : 2 * N + O],
                start=True,
                stop=False,
            )
            nc.tensor.matmul_mx(
                out=p_bank[:],
                lhsT=wb_codes[:, P * h : P * (h + 1)].bitcast(E4M3),
                lhsT_scale=second_plane[:, P * h : P * (h + 1)],
                rhs=hid_codes[:].bitcast(E5M2),
                rhs_scale=hid_scales[:],
                start=False,
                stop=True,
            )
            result = tile("result%d" % h, O, F32)
            nc.vector.tensor_tensor(result[:], p_bank[:], last_gate[:], MULT)
            queue = nc.sync if h == 0 else nc.scalar
            queue.dma_start(out[P * h : P * (h + 1), :], result[:])
